import numpy as np
import ml_dtypes


def mxq(x, axis, fmt="e4m3"):
    dtype, down = {"e4m3": (ml_dtypes.float8_e4m3fn, 7), "e5m2": (ml_dtypes.float8_e5m2, 14)}[fmt]
    v = np.moveaxis(np.asarray(x, np.float32).astype(ml_dtypes.bfloat16).astype(np.float64), axis, -1)
    blocks = v.reshape(v.shape[:-1] + (-1, 32))
    amax = np.abs(blocks).max(-1, keepdims=True)
    byte = np.maximum(np.where(amax > 0, np.frexp(amax)[1] - 1 + 127, 0) - down, 1)
    scale = np.exp2(byte - 127.0)
    codes = (blocks / scale).astype(np.float32).astype(dtype).astype(np.float64)
    return np.moveaxis((codes * scale).reshape(v.shape), -1, axis)


WIDE = False


def mx_kscale(k):
    if not WIDE:
        return np.ones(k)
    levels = np.array([10, -10, 5, -5, 0])
    if k % 512:
        return np.exp2(np.random.permutation(np.resize(levels, k // 32))).repeat(32)
    a = np.empty((k // 512, 16))
    for p in range(k // 512):
        a[p, :8] = np.random.permutation(np.resize(levels, 8))
        for g in range(8):
            far = levels[np.abs(levels - a[p, g]) >= 10]
            a[p, g + 8] = far[np.random.randint(len(far))]
    return np.exp2(a.ravel()).repeat(32)


def f64(x):
    return np.asarray(x).astype(np.float64)


def striped(idx):
    return np.tile(np.asarray(idx).reshape(-1, 16).T, (8, 1)).astype(np.uint16)


def unstriped(offs):
    return offs[:16].T.reshape(-1).astype(np.int64)


def striped8(idx):
    return np.asarray(idx).reshape(8, -1, 16).transpose(0, 2, 1).reshape(128, -1).astype(np.uint16)


def unstriped8(offs):
    return offs.reshape(8, 16, -1).transpose(0, 2, 1).reshape(8, -1).astype(np.int64)


def pick8(x, idx, run):
    r = np.arange(len(x))
    return x[r[:, None], idx[r % (8 * run) // run]]


E2M1 = np.array([0.0, 0.5, 1.0, 1.5, 2.0, 3.0, 4.0, 6.0, -0.0, -0.5, -1.0, -1.5, -2.0, -3.0, -4.0, -6.0])


def pack_weight(w, fmt):
    k, n = w.shape
    w = f64(np.asarray(w, np.float32).astype(ml_dtypes.bfloat16)).reshape(k // 32, 32, n)
    amax = np.abs(w).max(1)
    if fmt == "e4m3":
        byte = np.frexp(amax)[1] - 1 + 127 - 7
    else:
        mant, ex = np.frexp(amax / 6.0)
        byte = np.where(mant > 0.5, ex, ex - 1) + 127
    byte = np.clip(np.where(amax > 0, byte, 1), 1, 254)
    scaled = (w * np.exp2(127.0 - byte)[:, None, :]).reshape(k, n).astype(np.float32)
    by_word = np.ascontiguousarray(scaled.reshape(k // 512, 128, 4, n).transpose(0, 1, 3, 2))
    if fmt == "e4m3":
        words = by_word.astype(ml_dtypes.float8_e4m3fn).view(np.uint8)
    else:
        c = by_word.astype(ml_dtypes.float4_e2m1fn).view(np.uint8) & 0xF
        words = (c[..., 0::2] | (c[..., 1::2] << 4)).reshape(k // 512, 128, 2 * n)
    return np.ascontiguousarray(words), np.ascontiguousarray(byte.astype(np.uint8).reshape(k // 512, 16, n))


def unpack_weight(words, scales, fmt):
    g, _, n = scales.shape
    words = np.ascontiguousarray(words).reshape(g, 128, n, -1)
    if fmt == "e4m3":
        vals = words.view(ml_dtypes.float8_e4m3fn).astype(np.float64)
    else:
        nib = np.empty((g, 128, n, 4), np.uint8)
        nib[..., 0::2] = words & 0xF
        nib[..., 1::2] = words >> 4
        vals = E2M1[nib]
    vals = vals * np.repeat(np.exp2(scales.astype(np.float64) - 127.0), 8, axis=1)[..., None]
    return vals.transpose(0, 1, 3, 2).reshape(g * 512, n)


K, J, R, T, F, Z, M, O, C, N = 512, 256, 512, 512, 2048, 512, 1024, 128, 512, 256


def setup_inputs():
    n = np.random.standard_normal
    idx = np.stack([np.random.permutation(T)[:J] for _ in range(8)])
    idx2 = np.stack([np.random.permutation(F)[:R] for _ in range(8)])
    idx3 = np.stack([np.random.permutation(F)[:R] for _ in range(8)])
    idx4 = np.random.permutation(M)[:J]
    idx5 = np.stack([np.random.permutation(C)[:J] for _ in range(8)])
    idx6 = np.stack([np.random.permutation(C)[:O] for _ in range(8)])
    idx7 = np.stack([np.random.permutation(J)[:O] for _ in range(8)])
    fk = mx_kscale(K)
    fz = mx_kscale(Z)
    fr = mx_kscale(R)
    xop = pack_weight(n((Z, M)) / fz[:, None], "e2m1")
    w2p = pack_weight(n((Z, R)) * 1 / np.sqrt(Z) * fz[:, None], "e4m3")
    wbp = pack_weight(n((R, N)) * 1 / np.sqrt(R) / fr[:, None], "e4m3")
    return {
        "ta": (np.random.randint(-7, 8, (K, T)).astype(np.float64)).astype(np.float32),
        "ga": ((np.random.randint(8, 25, (K, 1)) / 64.0) * fk[:, None]).astype(np.float32),
        "ua": (np.random.randint(-7, 8, (K, F)).astype(np.float64)).astype(np.float32),
        "ha": ((np.random.randint(10, 25, (K, 1)) / 1024.0) / fk[:, None]).astype(np.float32),
        "hb": ((np.random.randint(4, 13, (K, 1)) / 1024.0) / fk[:, None]).astype(np.float32),
        "xo_words": xop[0],
        "xo_scales": xop[1],
        "w2_words": w2p[0],
        "w2_scales": w2p[1],
        "sa": (np.random.uniform(0.5, 1.6, (R, 1)) * fr[:, None]).astype(np.float32),
        "sb": (np.random.uniform(0.5, 1.6, (R, 1)) * fr[:, None]).astype(np.float32),
        "wb_words": wbp[0],
        "wb_scales": wbp[1],
        "offs": striped8(idx),
        "offs2": striped8(idx2),
        "offs3": striped8(idx3),
        "offs4": striped(idx4),
        "offs5": striped8(idx5),
        "offs6": striped8(idx6),
        "offs7": striped8(idx7),
    }


def reference(ta, ga, ua, ha, hb, xo_words, xo_scales, w2_words, w2_scales, sa, sb, wb_words, wb_scales, offs, offs2, offs3, offs4, offs5, offs6, offs7):
    idx = unstriped8(offs)
    idx2 = unstriped8(offs2)
    idx3 = unstriped8(offs3)
    idx4 = unstriped(offs4)
    idx5 = unstriped8(offs5)
    idx6 = unstriped8(offs6)
    idx7 = unstriped8(offs7)
    xou = unpack_weight(xo_words, xo_scales, "e2m1")
    w2u = unpack_weight(w2_words, w2_scales, "e4m3")
    wbu = unpack_weight(wb_words, wb_scales, "e4m3")
    xc = pick8(f64(ta), idx, 64) * f64(ga)
    wc = pick8(f64(ua), idx2, 64) * f64(ha) + pick8(f64(ua), idx3, 64) * f64(hb)
    wcq = mxq(wc, 0, "e4m3")
    xcq = mxq(xc, 0, "e4m3")
    a = wcq.T @ xcq
    xoidx4g = xou[:, idx4]
    b = w2u.T @ xoidx4g
    pw = np.zeros((R, C))
    pw[np.arange(R)[:, None], idx5[np.arange(R) % 512 // 64]] = a
    hid = np.maximum(pick8(pw, idx6, 64) * f64(sa), pick8(b, idx7, 64) * f64(sb))
    hidq = mxq(hid, 0, "e4m3")
    y = wbu.T @ hidq
    return y

@@ -1,0 +1,246 @@
+from contextlib import ExitStack
+
+import concourse.mybir as mybir
+
+K, J, R, T, F, Z, M, O, C, N = 512, 256, 512, 512, 2048, 512, 1024, 128, 512, 256
+FLOPS = 2 * (K * R * J + Z * R * J + R * N * O)
+
+F32 = mybir.dt.float32
+BF16 = mybir.dt.bfloat16
+I32 = mybir.dt.int32
+U32 = mybir.dt.uint32
+U16 = mybir.dt.uint16
+U8 = mybir.dt.uint8
+FP8X4 = mybir.dt.float8_e4m3fn_x4
+FP4X4 = mybir.dt.float4_e2m1fn_x4
+COPY = mybir.ActivationFunctionType.Copy
+ADD = mybir.AluOpType.add
+MAX = mybir.AluOpType.max
+
+P = 128
+PACK = 4
+HALF = J // 2
+LANES = 16
+
+
+def tile_picked_codes_refined_two_boardmeet_one_plain_kernel(
+    tc, ta, ga, ua, ha, hb, xo_words, xo_scales, w2_words, w2_scales, sa, sb,
+    wb_words, wb_scales, offs, offs2, offs3, offs4, offs5, offs6, offs7, out,
+):
+    nc = tc.nc
+
+    with ExitStack() as ctx:
+        keep = ctx.enter_context(tc.tile_pool(name="keep", bufs=1))
+        psum = ctx.enter_context(tc.psum_pool(name="psum", bufs=1))
+
+        def load_list(name, src):
+            t = keep.tile([P, src.shape[1]], U16, name=name)
+            nc.sync.dma_start(t[:], src)
+            return t
+
+        def load_column(name, src, eng):
+            t = keep.tile([P, PACK], F32, name=name)
+            eng.dma_start(t[:], src.rearrange("(p t) o -> p (t o)", t=PACK))
+            return t
+
+        def load_rows(name, src, t):
+            w = keep.tile([P, src.shape[1]], F32, name=name)
+            nc.sync.dma_start(w[:], src.rearrange("(p t) c -> t p c", t=PACK)[t])
+            return w
+
+        def load_scales(name, src, eng):
+            plane = keep.tile([P, src.shape[2]], U8, name=name, align_bytes=64)
+            nc.vector.memset(plane[:].bitcast(I32), 0)
+            for q in range(4):
+                eng.dma_start(plane[32 * q : 32 * q + 4, :].bitcast(I32), src[0][4 * q : 4 * q + 4, :].bitcast(I32))
+            return plane
+
+        def load_words(name, src):
+            words = keep.tile([P, src.shape[2]], U32, name=name, align_bytes=64)
+            nc.sync.dma_start(words[:].bitcast(I32), src[0].rearrange("p c r -> p (c r)").bitcast(I32))
+            return words
+
+        l2 = load_list("l2", offs2)
+        ha_t = load_column("ha_t", ha, nc.scalar)
+        ua_t = [load_rows("ua0", ua, 0)]
+        l3 = load_list("l3", offs3)
+        hb_t = load_column("hb_t", hb, nc.scalar)
+        ua_t.append(load_rows("ua1", ua, 1))
+        w2_s = load_scales("w2_s", w2_scales, nc.sync)
+        ua_t.append(load_rows("ua2", ua, 2))
+        l4 = load_list("l4", offs4)
+        l1 = load_list("l1", offs)
+        ua_t.append(load_rows("ua3", ua, 3))
+        xo_w = keep.tile([P, M], U16, name="xo_w", align_bytes=64)
+        nc.sync.dma_start(xo_w[:].bitcast(I32), xo_words[0].bitcast(I32))
+        xo_s = load_scales("xo_s", xo_scales, nc.sync)
+        ga_t = load_column("ga_t", ga, nc.sync)
+        ta_t = [load_rows("ta%d" % t, ta, t) for t in range(PACK)]
+        l5 = load_list("l5", offs5)
+        w2_w = load_words("w2_w", w2_words)
+        sb_t = load_column("sb_t", sb, nc.sync)
+        l7 = load_list("l7", offs7)
+        sa_t = load_column("sa_t", sa, nc.sync)
+        l6 = load_list("l6", offs6)
+        wb_w = load_words("wb_w", wb_words)
+
+        wb_s = load_scales("wb_s", wb_scales, nc.sync)
+
+        boards = [keep.tile([P, C], F32, name="board%d" % t) for t in range(PACK)]
+        for board in boards:
+            nc.vector.memset(board[:], 0.0)
+
+        wc_in = keep.tile([P, R * PACK], BF16, name="wc_in", align_bytes=64)
+        wc_pairs = keep.tile([P, R * PACK], BF16, name="wc_pairs", align_bytes=64)
+        wc_slots = wc_pairs[:].rearrange("p (g u m e) -> p g e m u", g=2, u=PACK, e=2)
+        for t in range(PACK):
+            coarse = keep.tile([P, R], F32, name="coarse%d" % t)
+            fine = keep.tile([P, R], F32, name="fine%d" % t)
+            nc.scalar.activation(coarse[:], ua_t[t][:].indirect(l2[:]), COPY, scale=ha_t[:, t : t + 1])
+            nc.scalar.activation(fine[:], ua_t[t][:].indirect(l3[:]), COPY, scale=hb_t[:, t : t + 1])
+            for half in range(2):
+                us = slice(2 * half, 2 * half + 2)
+                nc.vector.tensor_tensor(
+                    wc_slots[:, t // 2, t % 2, :, us],
+                    coarse[:].rearrange("p (m u) -> p m u", u=PACK)[:, :, us],
+                    fine[:].rearrange("p (m u) -> p m u", u=PACK)[:, :, us],
+                    ADD,
+                )
+        for half in range(2):
+            cols = slice(half * R // 2, (half + 1) * R // 2)
+            nc.vector.tensor_copy(
+                wc_in[:].bitcast(F32).rearrange("p (c g) -> p c g", g=2)[:, cols, :],
+                wc_pairs[:].bitcast(F32).rearrange("p (g c) -> p c g", g=2)[:, cols, :],
+            )
+
+        w2_sd = keep.tile([P, R], U8, name="w2_sd", align_bytes=64)
+        nc.vector.tensor_copy(
+            w2_sd[:].rearrange("p (u m) -> p u m", u=PACK), w2_s[:].rearrange("p (m u) -> p u m", u=PACK)
+        )
+        xo_g = keep.tile([P, J], U16, name="xo_g", align_bytes=64)
+        xo_gs = keep.tile([P, J], U8, name="xo_gs", align_bytes=64)
+        nc.vector.tensor_copy(xo_g[:], xo_w[:].indirect(l4[:]))
+        nc.vector.tensor_copy(xo_gs[:], xo_s[:].indirect(l4[:]))
+
+        wc_q = keep.tile([P, R], U32, name="wc_q", align_bytes=64)
+        wc_s = keep.tile([P, R], U8, name="wc_s", align_bytes=64)
+
+        def quantize_wc(half):
+            cols = slice(half * R // 2, (half + 1) * R // 2)
+            nc.vector.quantize_mx(
+                out=wc_q[:, cols].bitcast(FP8X4), scales=wc_s[:, cols],
+                in_=wc_in[:, PACK * cols.start : PACK * cols.stop],
+            )
+
+        def entries(lst, half):
+            return lst[:, half * HALF // LANES : (half + 1) * HALF // LANES]
+
+        def gather_xc(half):
+            rows = keep.tile([P, PACK, HALF], BF16, name="xc_rows%d" % half, tag="stage_a", align_bytes=64)
+            for t in range(PACK):
+                nc.scalar.activation(rows[:, t, :], ta_t[t][:].indirect(entries(l1, half)), COPY, scale=ga_t[:, t : t + 1])
+            return rows
+
+        def interleave_xc(half, rows, tag):
+            xc_in = keep.tile([P, HALF * PACK], BF16, name="xc_in%d" % half, tag=tag, align_bytes=64)
+            nc.scalar.copy(
+                xc_in[:].rearrange("p (c i t) -> p c t i", i=4, t=PACK),
+                rows[:].rearrange("p t (c i) -> p c t i", i=4),
+            )
+            return xc_in
+
+        def quantize_xc(half, xc_in):
+            codes = keep.tile([P, HALF], U32, name="xc_q%d" % half, align_bytes=64)
+            scales = keep.tile([P, HALF], U8, name="xc_s%d" % half, align_bytes=64)
+            nc.vector.quantize_mx(out=codes[:].bitcast(FP8X4), scales=scales[:], in_=xc_in[:])
+            return codes, scales
+
+        def product_a(acc, u, xq):
+            cols = slice(u * P, (u + 1) * P)
+            nc.tensor.matmul_mx(
+                out=acc, lhsT=wc_q[:, cols].bitcast(FP8X4), lhsT_scale=wc_s[:, cols],
+                rhs=xq[0][:].bitcast(FP8X4), rhs_scale=xq[1][:], start=True, stop=True,
+            )
+
+        def scatter(u, half, values):
+            nc.vector.tensor_copy(boards[u][:].indirect(entries(l5, half)), values)
+
+        rows0 = gather_xc(0)
+        xc_in0 = interleave_xc(0, rows0, "xc_in0")
+        quantize_wc(0)
+        xq0 = quantize_xc(0, xc_in0)
+        quantize_wc(1)
+        acc0 = psum.tile([P, HALF], F32, name="acc0")
+        acc1 = psum.tile([P, HALF], F32, name="acc1")
+        acc23 = psum.tile([P, 2, HALF], F32, name="acc23")
+        product_a(acc0[:], 0, xq0)
+        product_a(acc1[:], 1, xq0)
+        product_a(acc23[:, 0, :], 2, xq0)
+        product_a(acc23[:, 1, :], 3, xq0)
+        a0 = keep.tile([P, HALF], F32, name="a0", tag="stage_b", align_bytes=64)
+        nc.vector.tensor_copy(a0[:], acc0[:])
+        scatter(0, 0, a0[:])
+
+        rows1 = gather_xc(1)
+        a1 = keep.tile([P, HALF], F32, name="a1")
+        nc.scalar.copy(a1[:], acc1[:])
+        scatter(1, 0, a1[:])
+        xc_in1 = interleave_xc(1, rows1, "stage_b")
+        xq1 = quantize_xc(1, xc_in1)
+        a23 = keep.tile([P, 2, HALF], F32, name="a23", tag="stage_a", align_bytes=64)
+        nc.scalar.copy(a23[:], acc23[:])
+        scatter(2, 0, a23[:, 0, :])
+        scatter(3, 0, a23[:, 1, :])
+
+        acc_h1 = psum.tile([P, PACK, HALF], F32, name="acc_h1")
+        for u in range(PACK):
+            product_a(acc_h1[:, u, :], u, xq1)
+        a_h1 = keep.tile([P, PACK, HALF], F32, name="a_h1")
+        nc.scalar.copy(a_h1[:], acc_h1[:])
+        for u in range(PACK):
+            scatter(u, 1, a_h1[:, u, :])
+
+        w2_d = keep.tile([P, R], U32, name="w2_d", align_bytes=64)
+        nc.scalar.copy(
+            w2_d[:].rearrange("p (u m) -> p m u", u=PACK), w2_w[:].rearrange("p (m u) -> p m u", u=PACK)
+        )
+        acc_b = [psum.tile([P, 2, J], F32, name="acc_b%d" % i) for i in range(2)]
+        b_pick = keep.tile([P, PACK, O], F32, name="b_pick")
+        for u in range(PACK):
+            cols = slice(u * P, (u + 1) * P)
+            acc = acc_b[u // 2][:, u % 2, :]
+            nc.tensor.matmul_mx(
+                out=acc, lhsT=w2_d[:, cols].bitcast(FP8X4), lhsT_scale=w2_sd[:, cols],
+                rhs=xo_g[:].bitcast(FP4X4), rhs_scale=xo_gs[:], start=True, stop=True,
+            )
+        for u in range(PACK):
+            b_rows = keep.tile([P, J], F32, name="b_rows%d" % u)
+            nc.scalar.copy(b_rows[:], acc_b[u // 2][:, u % 2, :])
+            nc.scalar.activation(b_pick[:, u, :], b_rows[:].indirect(l7[:]), COPY, scale=sb_t[:, u : u + 1])
+
+        a_pick = keep.tile([P, PACK, O], F32, name="a_pick")
+        for u in range(PACK):
+            nc.scalar.activation(a_pick[:, u, :], boards[u][:].indirect(l6[:]), COPY, scale=sa_t[:, u : u + 1])
+        hid_in = keep.tile([P, O * PACK], BF16, name="hid_in", align_bytes=64)
+        hid_slots = hid_in[:].rearrange("p (o u) -> p o u", u=PACK)
+        for slots in (slice(0, PACK - 1), slice(PACK - 1, PACK)):
+            nc.vector.tensor_tensor(
+                hid_slots[:, :, slots],
+                a_pick[:, slots, :].rearrange("p u o -> p o u"),
+                b_pick[:, slots, :].rearrange("p u o -> p o u"),
+                MAX,
+            )
+        hid_q = keep.tile([P, O], U32, name="hid_q", align_bytes=64)
+        hid_s = keep.tile([P, O], U8, name="hid_s", align_bytes=64)
+        nc.vector.quantize_mx(out=hid_q[:].bitcast(FP8X4), scales=hid_s[:], in_=hid_in[:])
+
+        for h, (copy, queue) in enumerate(((nc.vector.tensor_copy, nc.sync), (nc.scalar.copy, nc.scalar))):
+            cols = slice(h * P, (h + 1) * P)
+            acc_y = psum.tile([P, O], F32, name="acc_y%d" % h)
+            nc.tensor.matmul_mx(
+                out=acc_y[:], lhsT=wb_w[:, cols].bitcast(FP8X4), lhsT_scale=wb_s[:, cols],
+                rhs=hid_q[:].bitcast(FP8X4), rhs_scale=hid_s[:], start=True, stop=True,
+            )
+            y = keep.tile([P, O], F32, name="y%d" % h)
+            copy(y[:], acc_y[:])
+            queue.dma_start(out[cols, :], y[:])

@@ -60,6 +60,11 @@ def tile_picked_codes_refined_two_boardmeet_one_plain_kernel(
             nc.sync.dma_start(words[:].bitcast(I32), src[0].rearrange("p c r -> p (c r)").bitcast(I32))
             return words
 
+        warm_in = keep.tile([P, 1], F32, name="warm_in")
+        warm_out = keep.tile([P, 1], F32, name="warm_out")
+        nc.gpsimd.memset(warm_in[:], 0.0)
+        nc.scalar.activation(warm_out[:], warm_in[:], COPY)
+
         l2 = load_list("l2", offs2)
         ha_t = load_column("ha_t", ha, nc.scalar)
         ua_t = [load_rows("ua0", ua, 0)]

@@ -56,7 +56,7 @@ def tile_picked_codes_refined_two_boardmeet_one_plain_kernel(
             return plane
 
         def load_words(name, src):
-            words = keep.tile([P, src.shape[2]], U32, name=name, align_bytes=64)
+            words = keep.tile([P, src.shape[2]], U32, name=name, tag=name, align_bytes=64)
             nc.sync.dma_start(words[:].bitcast(I32), src[0].rearrange("p c r -> p (c r)").bitcast(I32))
             return words
 
@@ -65,9 +65,9 @@ def tile_picked_codes_refined_two_boardmeet_one_plain_kernel(
         nc.gpsimd.memset(warm_in[:], 0.0)
         nc.scalar.activation(warm_out[:], warm_in[:], COPY)
 
+        ua_t = [load_rows("ua0", ua, 0)]
         l2 = load_list("l2", offs2)
         ha_t = load_column("ha_t", ha, nc.scalar)
-        ua_t = [load_rows("ua0", ua, 0)]
         l3 = load_list("l3", offs3)
         hb_t = load_column("hb_t", hb, nc.scalar)
         ua_t.append(load_rows("ua1", ua, 1))
@@ -175,14 +175,19 @@ def tile_picked_codes_refined_two_boardmeet_one_plain_kernel(
         quantize_wc(0)
         xq0 = quantize_xc(0, xc_in0)
         quantize_wc(1)
-        acc0 = psum.tile([P, HALF], F32, name="acc0")
+        acc0 = psum.tile([P, HALF], F32, name="acc0", tag="bank_first")
         acc1 = psum.tile([P, HALF], F32, name="acc1")
         acc23 = psum.tile([P, 2, HALF], F32, name="acc23")
         product_a(acc0[:], 0, xq0)
         product_a(acc1[:], 1, xq0)
         product_a(acc23[:, 0, :], 2, xq0)
         product_a(acc23[:, 1, :], 3, xq0)
-        a0 = keep.tile([P, HALF], F32, name="a0", tag="stage_b", align_bytes=64)
+        w2_d = keep.tile([P, R], U32, name="w2_d", tag="xc_in0", align_bytes=64)
+        nc.vector.tensor_copy(
+            w2_d[:].bitcast(I32).rearrange("p (u m) -> p m u", u=PACK),
+            w2_w[:].bitcast(I32).rearrange("p (m u) -> p m u", u=PACK),
+        )
+        a0 = keep.tile([P, HALF], F32, name="a0")
         nc.vector.tensor_copy(a0[:], acc0[:])
         scatter(0, 0, a0[:])
 
@@ -190,38 +195,38 @@ def tile_picked_codes_refined_two_boardmeet_one_plain_kernel(
         a1 = keep.tile([P, HALF], F32, name="a1")
         nc.scalar.copy(a1[:], acc1[:])
         scatter(1, 0, a1[:])
-        xc_in1 = interleave_xc(1, rows1, "stage_b")
+        xc_in1 = interleave_xc(1, rows1, "w2_w")
         xq1 = quantize_xc(1, xc_in1)
         a23 = keep.tile([P, 2, HALF], F32, name="a23", tag="stage_a", align_bytes=64)
         nc.scalar.copy(a23[:], acc23[:])
         scatter(2, 0, a23[:, 0, :])
         scatter(3, 0, a23[:, 1, :])
 
-        acc_h1 = psum.tile([P, PACK, HALF], F32, name="acc_h1")
-        for u in range(PACK):
-            product_a(acc_h1[:, u, :], u, xq1)
+        acc_h1_0 = psum.tile([P, HALF], F32, name="acc_h1_0", tag="bank_first")
+        acc_h1 = psum.tile([P, PACK - 1, HALF], F32, name="acc_h1")
+        product_a(acc_h1_0[:], 0, xq1)
+        for u in range(1, PACK):
+            product_a(acc_h1[:, u - 1, :], u, xq1)
         a_h1 = keep.tile([P, PACK, HALF], F32, name="a_h1")
-        nc.scalar.copy(a_h1[:], acc_h1[:])
+        nc.scalar.copy(a_h1[:, 0, :], acc_h1_0[:])
+        nc.scalar.copy(a_h1[:, 1:PACK, :], acc_h1[:])
         for u in range(PACK):
             scatter(u, 1, a_h1[:, u, :])
 
-        w2_d = keep.tile([P, R], U32, name="w2_d", align_bytes=64)
-        nc.scalar.copy(
-            w2_d[:].rearrange("p (u m) -> p m u", u=PACK), w2_w[:].rearrange("p (m u) -> p m u", u=PACK)
-        )
-        acc_b = [psum.tile([P, 2, J], F32, name="acc_b%d" % i) for i in range(2)]
         b_pick = keep.tile([P, PACK, O], F32, name="b_pick")
+        b_rows = [keep.tile([P, J], F32, name="b_rows%d" % u) for u in range(PACK)]
+        for pair in range(2):
+            acc_b = psum.tile([P, 2, J], F32, name="acc_b%d" % pair)
+            for e in range(2):
+                cols = slice((2 * pair + e) * P, (2 * pair + e + 1) * P)
+                nc.tensor.matmul_mx(
+                    out=acc_b[:, e, :], lhsT=w2_d[:, cols].bitcast(FP8X4), lhsT_scale=w2_sd[:, cols],
+                    rhs=xo_g[:].bitcast(FP4X4), rhs_scale=xo_gs[:], start=True, stop=True,
+                )
+            for e in range(2):
+                nc.scalar.copy(b_rows[2 * pair + e][:], acc_b[:, e, :])
         for u in range(PACK):
-            cols = slice(u * P, (u + 1) * P)
-            acc = acc_b[u // 2][:, u % 2, :]
-            nc.tensor.matmul_mx(
-                out=acc, lhsT=w2_d[:, cols].bitcast(FP8X4), lhsT_scale=w2_sd[:, cols],
-                rhs=xo_g[:].bitcast(FP4X4), rhs_scale=xo_gs[:], start=True, stop=True,
-            )
-        for u in range(PACK):
-            b_rows = keep.tile([P, J], F32, name="b_rows%d" % u)
-            nc.scalar.copy(b_rows[:], acc_b[u // 2][:, u % 2, :])
-            nc.scalar.activation(b_pick[:, u, :], b_rows[:].indirect(l7[:]), COPY, scale=sb_t[:, u : u + 1])
+            nc.scalar.activation(b_pick[:, u, :], b_rows[u][:].indirect(l7[:]), COPY, scale=sb_t[:, u : u + 1])
 
         a_pick = keep.tile([P, PACK, O], F32, name="a_pick")
         for u in range(PACK):

from contextlib import ExitStack

import concourse.mybir as mybir

K, J, R, T, F, Z, M, O, C, N = 512, 256, 512, 512, 2048, 512, 1024, 128, 512, 256
FLOPS = 2 * (K * R * J + Z * R * J + R * N * O)

F32 = mybir.dt.float32
BF16 = mybir.dt.bfloat16
I32 = mybir.dt.int32
U32 = mybir.dt.uint32
U16 = mybir.dt.uint16
U8 = mybir.dt.uint8
FP8X4 = mybir.dt.float8_e4m3fn_x4
FP4X4 = mybir.dt.float4_e2m1fn_x4
COPY = mybir.ActivationFunctionType.Copy
ADD = mybir.AluOpType.add
MAX = mybir.AluOpType.max

P = 128
PACK = 4
HALF = J // 2
LANES = 16


def tile_picked_codes_refined_two_boardmeet_one_plain_kernel(
    tc, ta, ga, ua, ha, hb, xo_words, xo_scales, w2_words, w2_scales, sa, sb,
    wb_words, wb_scales, offs, offs2, offs3, offs4, offs5, offs6, offs7, out,
):
    nc = tc.nc

    with ExitStack() as ctx:
        keep = ctx.enter_context(tc.tile_pool(name="keep", bufs=1))
        psum = ctx.enter_context(tc.psum_pool(name="psum", bufs=1))

        def load_list(name, src):
            t = keep.tile([P, src.shape[1]], U16, name=name)
            nc.sync.dma_start(t[:], src)
            return t

        def load_column(name, src, eng):
            t = keep.tile([P, PACK], F32, name=name)
            eng.dma_start(t[:], src.rearrange("(p t) o -> p (t o)", t=PACK))
            return t

        def load_rows(name, src, t):
            w = keep.tile([P, src.shape[1]], F32, name=name)
            nc.sync.dma_start(w[:], src.rearrange("(p t) c -> t p c", t=PACK)[t])
            return w

        def load_scales(name, src, eng):
            plane = keep.tile([P, src.shape[2]], U8, name=name, align_bytes=64)
            nc.vector.memset(plane[:].bitcast(I32), 0)
            for q in range(4):
                eng.dma_start(plane[32 * q : 32 * q + 4, :].bitcast(I32), src[0][4 * q : 4 * q + 4, :].bitcast(I32))
            return plane

        def load_words(name, src):
            words = keep.tile([P, src.shape[2]], U32, name=name, tag=name, align_bytes=64)
            nc.sync.dma_start(words[:].bitcast(I32), src[0].rearrange("p c r -> p (c r)").bitcast(I32))
            return words

        warm_in = keep.tile([P, 1], F32, name="warm_in")
        warm_out = keep.tile([P, 1], F32, name="warm_out")
        nc.gpsimd.memset(warm_in[:], 0.0)
        nc.scalar.activation(warm_out[:], warm_in[:], COPY)

        ua_t = [load_rows("ua0", ua, 0)]
        l2 = load_list("l2", offs2)
        ha_t = load_column("ha_t", ha, nc.scalar)
        l3 = load_list("l3", offs3)
        hb_t = load_column("hb_t", hb, nc.scalar)
        ua_t.append(load_rows("ua1", ua, 1))
        w2_s = load_scales("w2_s", w2_scales, nc.sync)
        ua_t.append(load_rows("ua2", ua, 2))
        l4 = load_list("l4", offs4)
        l1 = load_list("l1", offs)
        ua_t.append(load_rows("ua3", ua, 3))
        xo_w = keep.tile([P, M], U16, name="xo_w", align_bytes=64)
        nc.sync.dma_start(xo_w[:].bitcast(I32), xo_words[0].bitcast(I32))
        xo_s = load_scales("xo_s", xo_scales, nc.sync)
        ga_t = load_column("ga_t", ga, nc.sync)
        ta_t = [load_rows("ta%d" % t, ta, t) for t in range(PACK)]
        l5 = load_list("l5", offs5)
        w2_w = load_words("w2_w", w2_words)
        sb_t = load_column("sb_t", sb, nc.sync)
        l7 = load_list("l7", offs7)
        sa_t = load_column("sa_t", sa, nc.sync)
        l6 = load_list("l6", offs6)
        wb_w = load_words("wb_w", wb_words)

        wb_s = load_scales("wb_s", wb_scales, nc.sync)

        boards = [keep.tile([P, C], F32, name="board%d" % t) for t in range(PACK)]
        for board in boards:
            nc.vector.memset(board[:], 0.0)

        wc_in = keep.tile([P, R * PACK], BF16, name="wc_in", align_bytes=64)
        wc_pairs = keep.tile([P, R * PACK], BF16, name="wc_pairs", align_bytes=64)
        wc_slots = wc_pairs[:].rearrange("p (g u m e) -> p g e m u", g=2, u=PACK, e=2)
        for t in range(PACK):
            coarse = keep.tile([P, R], F32, name="coarse%d" % t)
            fine = keep.tile([P, R], F32, name="fine%d" % t)
            nc.scalar.activation(coarse[:], ua_t[t][:].indirect(l2[:]), COPY, scale=ha_t[:, t : t + 1])
            nc.scalar.activation(fine[:], ua_t[t][:].indirect(l3[:]), COPY, scale=hb_t[:, t : t + 1])
            for half in range(2):
                us = slice(2 * half, 2 * half + 2)
                nc.vector.tensor_tensor(
                    wc_slots[:, t // 2, t % 2, :, us],
                    coarse[:].rearrange("p (m u) -> p m u", u=PACK)[:, :, us],
                    fine[:].rearrange("p (m u) -> p m u", u=PACK)[:, :, us],
                    ADD,
                )
        for half in range(2):
            cols = slice(half * R // 2, (half + 1) * R // 2)
            nc.vector.tensor_copy(
                wc_in[:].bitcast(F32).rearrange("p (c g) -> p c g", g=2)[:, cols, :],
                wc_pairs[:].bitcast(F32).rearrange("p (g c) -> p c g", g=2)[:, cols, :],
            )

        w2_sd = keep.tile([P, R], U8, name="w2_sd", align_bytes=64)
        nc.vector.tensor_copy(
            w2_sd[:].rearrange("p (u m) -> p u m", u=PACK), w2_s[:].rearrange("p (m u) -> p u m", u=PACK)
        )
        xo_g = keep.tile([P, J], U16, name="xo_g", align_bytes=64)
        xo_gs = keep.tile([P, J], U8, name="xo_gs", align_bytes=64)
        nc.vector.tensor_copy(xo_g[:], xo_w[:].indirect(l4[:]))
        nc.vector.tensor_copy(xo_gs[:], xo_s[:].indirect(l4[:]))

        wc_q = keep.tile([P, R], U32, name="wc_q", align_bytes=64)
        wc_s = keep.tile([P, R], U8, name="wc_s", align_bytes=64)

        def quantize_wc(half):
            cols = slice(half * R // 2, (half + 1) * R // 2)
            nc.vector.quantize_mx(
                out=wc_q[:, cols].bitcast(FP8X4), scales=wc_s[:, cols],
                in_=wc_in[:, PACK * cols.start : PACK * cols.stop],
            )

        def entries(lst, half):
            return lst[:, half * HALF // LANES : (half + 1) * HALF // LANES]

        def gather_xc(half):
            rows = keep.tile([P, PACK, HALF], BF16, name="xc_rows%d" % half, tag="stage_a", align_bytes=64)
            for t in range(PACK):
                nc.scalar.activation(rows[:, t, :], ta_t[t][:].indirect(entries(l1, half)), COPY, scale=ga_t[:, t : t + 1])
            return rows

        def interleave_xc(half, rows, tag):
            xc_in = keep.tile([P, HALF * PACK], BF16, name="xc_in%d" % half, tag=tag, align_bytes=64)
            nc.scalar.copy(
                xc_in[:].rearrange("p (c i t) -> p c t i", i=4, t=PACK),
                rows[:].rearrange("p t (c i) -> p c t i", i=4),
            )
            return xc_in

        def quantize_xc(half, xc_in):
            codes = keep.tile([P, HALF], U32, name="xc_q%d" % half, align_bytes=64)
            scales = keep.tile([P, HALF], U8, name="xc_s%d" % half, align_bytes=64)
            nc.vector.quantize_mx(out=codes[:].bitcast(FP8X4), scales=scales[:], in_=xc_in[:])
            return codes, scales

        def product_a(acc, u, xq):
            cols = slice(u * P, (u + 1) * P)
            nc.tensor.matmul_mx(
                out=acc, lhsT=wc_q[:, cols].bitcast(FP8X4), lhsT_scale=wc_s[:, cols],
                rhs=xq[0][:].bitcast(FP8X4), rhs_scale=xq[1][:], start=True, stop=True,
            )

        def scatter(u, half, values):
            nc.vector.tensor_copy(boards[u][:].indirect(entries(l5, half)), values)

        rows0 = gather_xc(0)
        xc_in0 = interleave_xc(0, rows0, "xc_in0")
        quantize_wc(0)
        xq0 = quantize_xc(0, xc_in0)
        quantize_wc(1)
        acc0 = psum.tile([P, HALF], F32, name="acc0", tag="bank_first")
        acc1 = psum.tile([P, HALF], F32, name="acc1")
        acc23 = psum.tile([P, 2, HALF], F32, name="acc23")
        product_a(acc0[:], 0, xq0)
        product_a(acc1[:], 1, xq0)
        product_a(acc23[:, 0, :], 2, xq0)
        product_a(acc23[:, 1, :], 3, xq0)
        w2_d = keep.tile([P, R], U32, name="w2_d", tag="xc_in0", align_bytes=64)
        nc.vector.tensor_copy(
            w2_d[:].bitcast(I32).rearrange("p (u m) -> p m u", u=PACK),
            w2_w[:].bitcast(I32).rearrange("p (m u) -> p m u", u=PACK),
        )
        a0 = keep.tile([P, HALF], F32, name="a0")
        nc.vector.tensor_copy(a0[:], acc0[:])
        scatter(0, 0, a0[:])

        rows1 = gather_xc(1)
        a1 = keep.tile([P, HALF], F32, name="a1")
        nc.scalar.copy(a1[:], acc1[:])
        scatter(1, 0, a1[:])
        xc_in1 = interleave_xc(1, rows1, "w2_w")
        xq1 = quantize_xc(1, xc_in1)
        a23 = keep.tile([P, 2, HALF], F32, name="a23", tag="stage_a", align_bytes=64)
        nc.scalar.copy(a23[:], acc23[:])
        scatter(2, 0, a23[:, 0, :])
        scatter(3, 0, a23[:, 1, :])

        acc_h1_0 = psum.tile([P, HALF], F32, name="acc_h1_0", tag="bank_first")
        acc_h1 = psum.tile([P, PACK - 1, HALF], F32, name="acc_h1")
        product_a(acc_h1_0[:], 0, xq1)
        for u in range(1, PACK):
            product_a(acc_h1[:, u - 1, :], u, xq1)
        a_h1 = keep.tile([P, PACK, HALF], F32, name="a_h1")
        nc.scalar.copy(a_h1[:, 0, :], acc_h1_0[:])
        nc.scalar.copy(a_h1[:, 1:PACK, :], acc_h1[:])
        for u in range(PACK):
            scatter(u, 1, a_h1[:, u, :])

        b_pick = keep.tile([P, PACK, O], F32, name="b_pick")
        b_rows = [keep.tile([P, J], F32, name="b_rows%d" % u) for u in range(PACK)]
        for pair in range(2):
            acc_b = psum.tile([P, 2, J], F32, name="acc_b%d" % pair)
            for e in range(2):
                cols = slice((2 * pair + e) * P, (2 * pair + e + 1) * P)
                nc.tensor.matmul_mx(
                    out=acc_b[:, e, :], lhsT=w2_d[:, cols].bitcast(FP8X4), lhsT_scale=w2_sd[:, cols],
                    rhs=xo_g[:].bitcast(FP4X4), rhs_scale=xo_gs[:], start=True, stop=True,
                )
            for e in range(2):
                nc.scalar.copy(b_rows[2 * pair + e][:], acc_b[:, e, :])
        for u in range(PACK):
            nc.scalar.activation(b_pick[:, u, :], b_rows[u][:].indirect(l7[:]), COPY, scale=sb_t[:, u : u + 1])

        a_pick = keep.tile([P, PACK, O], F32, name="a_pick")
        for u in range(PACK):
            nc.scalar.activation(a_pick[:, u, :], boards[u][:].indirect(l6[:]), COPY, scale=sa_t[:, u : u + 1])
        hid_in = keep.tile([P, O * PACK], BF16, name="hid_in", align_bytes=64)
        hid_slots = hid_in[:].rearrange("p (o u) -> p o u", u=PACK)
        for slots in (slice(0, PACK - 1), slice(PACK - 1, PACK)):
            nc.vector.tensor_tensor(
                hid_slots[:, :, slots],
                a_pick[:, slots, :].rearrange("p u o -> p o u"),
                b_pick[:, slots, :].rearrange("p u o -> p o u"),
                MAX,
            )
        hid_q = keep.tile([P, O], U32, name="hid_q", align_bytes=64)
        hid_s = keep.tile([P, O], U8, name="hid_s", align_bytes=64)
        nc.vector.quantize_mx(out=hid_q[:].bitcast(FP8X4), scales=hid_s[:], in_=hid_in[:])

        for h, (copy, queue) in enumerate(((nc.vector.tensor_copy, nc.sync), (nc.scalar.copy, nc.scalar))):
            cols = slice(h * P, (h + 1) * P)
            acc_y = psum.tile([P, O], F32, name="acc_y%d" % h)
            nc.tensor.matmul_mx(
                out=acc_y[:], lhsT=wb_w[:, cols].bitcast(FP8X4), lhsT_scale=wb_s[:, cols],
                rhs=hid_q[:].bitcast(FP8X4), rhs_scale=hid_s[:], start=True, stop=True,
            )
            y = keep.tile([P, O], F32, name="y%d" % h)
            copy(y[:], acc_y[:])
            queue.dma_start(out[cols, :], y[:])
